import numpy as np
import ml_dtypes


def mxq(x, axis, fmt="e4m3"):
    dtype, down = {"e4m3": (ml_dtypes.float8_e4m3fn, 7), "e5m2": (ml_dtypes.float8_e5m2, 14)}[fmt]
    v = np.moveaxis(np.asarray(x, np.float32).astype(ml_dtypes.bfloat16).astype(np.float64), axis, -1)
    blocks = v.reshape(v.shape[:-1] + (-1, 32))
    amax = np.abs(blocks).max(-1, keepdims=True)
    byte = np.maximum(np.where(amax > 0, np.frexp(amax)[1] - 1 + 127, 0) - down, 1)
    scale = np.exp2(byte - 127.0)
    codes = (blocks / scale).astype(np.float32).astype(dtype).astype(np.float64)
    return np.moveaxis((codes * scale).reshape(v.shape), -1, axis)


WIDE = False


def mx_kscale(k):
    if not WIDE:
        return np.ones(k)
    levels = np.array([10, -10, 5, -5, 0])
    if k % 512:
        return np.exp2(np.random.permutation(np.resize(levels, k // 32))).repeat(32)
    a = np.empty((k // 512, 16))
    for p in range(k // 512):
        a[p, :8] = np.random.permutation(np.resize(levels, 8))
        for g in range(8):
            far = levels[np.abs(levels - a[p, g]) >= 10]
            a[p, g + 8] = far[np.random.randint(len(far))]
    return np.exp2(a.ravel()).repeat(32)


def f64(x):
    return np.asarray(x).astype(np.float64)


def striped(idx):
    return np.tile(np.asarray(idx).reshape(-1, 16).T, (8, 1)).astype(np.uint16)


def unstriped(offs):
    return offs[:16].T.reshape(-1).astype(np.int64)


E2M1 = np.array([0.0, 0.5, 1.0, 1.5, 2.0, 3.0, 4.0, 6.0, -0.0, -0.5, -1.0, -1.5, -2.0, -3.0, -4.0, -6.0])


def pack_weight(w, fmt):
    k, n = w.shape
    w = f64(np.asarray(w, np.float32).astype(ml_dtypes.bfloat16)).reshape(k // 32, 32, n)
    amax = np.abs(w).max(1)
    if fmt == "e4m3":
        byte = np.frexp(amax)[1] - 1 + 127 - 7
    else:
        mant, ex = np.frexp(amax / 6.0)
        byte = np.where(mant > 0.5, ex, ex - 1) + 127
    byte = np.clip(np.where(amax > 0, byte, 1), 1, 254)
    scaled = (w * np.exp2(127.0 - byte)[:, None, :]).reshape(k, n).astype(np.float32)
    by_word = np.ascontiguousarray(scaled.reshape(k // 512, 128, 4, n).transpose(0, 1, 3, 2))
    if fmt == "e4m3":
        words = by_word.astype(ml_dtypes.float8_e4m3fn).view(np.uint8)
    else:
        c = by_word.astype(ml_dtypes.float4_e2m1fn).view(np.uint8) & 0xF
        words = (c[..., 0::2] | (c[..., 1::2] << 4)).reshape(k // 512, 128, 2 * n)
    return np.ascontiguousarray(words), np.ascontiguousarray(byte.astype(np.uint8).reshape(k // 512, 16, n))


def unpack_weight(words, scales, fmt):
    g, _, n = scales.shape
    words = np.ascontiguousarray(words).reshape(g, 128, n, -1)
    if fmt == "e4m3":
        vals = words.view(ml_dtypes.float8_e4m3fn).astype(np.float64)
    else:
        nib = np.empty((g, 128, n, 4), np.uint8)
        nib[..., 0::2] = words & 0xF
        nib[..., 1::2] = words >> 4
        vals = E2M1[nib]
    vals = vals * np.repeat(np.exp2(scales.astype(np.float64) - 127.0), 8, axis=1)[..., None]
    return vals.transpose(0, 1, 3, 2).reshape(g * 512, n)


D, E, T, I, Q = 512, 512, 2048, 512, 128


def setup_inputs():
    n = np.random.standard_normal
    idx = np.random.permutation(T)[:I]
    fd = mx_kscale(D)
    fe = mx_kscale(E)
    keysp = pack_weight(n((D, T)) / fd[:, None], "e2m1")
    valsp = pack_weight(n((E, T)) / fe[:, None], "e2m1")
    return {
        "query": (n((D, Q)) * 0.5 / np.sqrt(D) * fd[:, None]).astype(np.float32),
        "keys_words": keysp[0],
        "keys_scales": keysp[1],
        "counts": (np.random.uniform(0.0, 2.0, (Q, T))).astype(np.float32),
        "weary": (np.random.uniform(0.3, 1.0, (Q, 1))).astype(np.float32),
        "gout": (n((E, Q)) * 1 / np.sqrt(E) * fe[:, None]).astype(np.float32),
        "vals_words": valsp[0],
        "vals_scales": valsp[1],
        "lse": (np.random.uniform(5.6, 6.0, (Q, 1))).astype(np.float32),
        "delta": (np.random.uniform(-0.3, 0.3, (Q, 1))).astype(np.float32),
        "later": (0.5 * n((Q, T))).astype(np.float32),
        "offs": striped(idx),
    }


def reference(query, keys_words, keys_scales, counts, weary, gout, vals_words, vals_scales, lse, delta, later, offs):
    idx = unstriped(offs)
    keysu = unpack_weight(keys_words, keys_scales, "e2m1")
    valsu = unpack_weight(vals_words, vals_scales, "e2m1")
    queryq = mxq(f64(query), 0, "e4m3")
    keysidxg = keysu[:, idx]
    a = queryq.T @ keysidxg
    goutq = mxq(f64(gout), 0, "e4m3")
    valsidxg = valsu[:, idx]
    dp = goutq.T @ valsidxg
    ds = np.exp(a - f64(counts)[:, idx] * f64(weary) - f64(lse)) * (dp - f64(delta)) * f64(weary) * (-512.0)
    df = np.zeros((Q, T))
    df[:, idx] = ds
    y = f64(later) + df
    return y

@@ -1,0 +1,158 @@
+from contextlib import ExitStack
+
+import concourse.mybir as mybir
+
+D, E, T, I, Q = 512, 512, 2048, 512, 128
+FLOPS = 2 * Q * I * (D + E)
+
+F32 = mybir.dt.float32
+BF16 = mybir.dt.bfloat16
+I32 = mybir.dt.int32
+U32 = mybir.dt.uint32
+U16 = mybir.dt.uint16
+U8 = mybir.dt.uint8
+FP8X4 = mybir.dt.float8_e4m3fn_x4
+FP4X4 = mybir.dt.float4_e2m1fn_x4
+ALU = mybir.AluOpType
+ACT = mybir.ActivationFunctionType
+
+P = 128
+PACK = 4
+HALF = I // 2
+OUT_WIDTHS = (512, 512, 512, 512)
+
+
+def tile_attend_gweariness_kernel(
+    tc, query, keys_words, keys_scales, counts, weary, gout, vals_words, vals_scales, lse, delta, later, offs, out
+):
+    nc = tc.nc
+    with ExitStack() as ctx:
+        sb = ctx.enter_context(tc.tile_pool(name="sb", bufs=1))
+        ps = ctx.enter_context(tc.psum_pool(name="ps", bufs=1))
+
+        offsets = sb.tile([P, I // 16], U16, name="offsets")
+        nc.sync.dma_start(offsets[:], offs)
+
+        def load_scales(src, name):
+            pool_scales = sb.tile([P, T], U8, name=name)
+            nc.vector.memset(pool_scales[:].bitcast(I32), 0)
+            rows = src[0].bitcast(I32)
+            for r in range(4):
+                nc.sync.dma_start(pool_scales[:].bitcast(I32)[r:P:32, :], rows[r:16:4, :])
+            return pool_scales
+
+        def load_words(src, name):
+            pool_words = sb.tile([P, T], U16, name=name)
+            nc.sync.dma_start(pool_words[:].bitcast(I32), src[0].bitcast(I32))
+            return pool_words
+
+        def load_rows(src, name):
+            raw = sb.tile([P, PACK, Q], F32, name=name)
+            nc.sync.dma_start(raw[:], src.rearrange("(p j) q -> p j q", j=PACK))
+            return raw
+
+        def load_column(src, name):
+            col = sb.tile([P, 1], F32, name=name)
+            nc.sync.dma_start(col[:], src)
+            return col
+
+        warm = sb.tile([P, 1], F32, name="warm")
+        nc.gpsimd.memset(warm[:], 0.0)
+        warm_out = sb.tile([P, 1], F32, name="warm_out")
+        nc.scalar.activation(warm_out[:], warm[:], ACT.Exp)
+
+        vs_pool = load_scales(vals_scales, "vs_pool")
+        vw_pool = load_words(vals_words, "vw_pool")
+        ks_pool = load_scales(keys_scales, "ks_pool")
+        g_raw = load_rows(gout, "g_raw")
+        kw_pool = load_words(keys_words, "kw_pool")
+        q_raw = load_rows(query, "q_raw")
+        w_col = load_column(weary, "w_col")
+        delta_col = load_column(delta, "delta_col")
+        lse_col = load_column(lse, "lse_col")
+        counts_pool = sb.tile([P, T], F32, name="counts_pool")
+        nc.sync.dma_start(counts_pool[:], counts)
+        later_sb = sb.tile([P, T], F32, name="later_sb")
+        nc.sync.dma_start(later_sb[:], later)
+
+        df = sb.tile([P, T], F32, name="df")
+        nc.vector.memset(df[:], 0.0)
+
+        def gather(pool_tile, dtype, name):
+            picked = sb.tile([P, I], dtype, name=name, align_bytes=64)
+            nc.vector.tensor_copy(picked[:], pool_tile[:].indirect(offsets[:]))
+            return picked
+
+        def interleave(raw, name):
+            grouped = sb.tile([P, Q, PACK], BF16, name=name, align_bytes=64)
+            nc.scalar.copy(grouped[:], raw[:].rearrange("p j q -> p q j"))
+            return grouped
+
+        def quantize(grouped, name):
+            codes = sb.tile([P, Q], U32, name=name + "_codes", align_bytes=64)
+            scales = sb.tile([P, Q], U8, name=name + "_scales", align_bytes=64)
+            nc.vector.quantize_mx(
+                out=codes[:].bitcast(FP8X4), scales=scales[:], in_=grouped[:].rearrange("p q j -> p (q j)")
+            )
+            return codes, scales
+
+        def product(codes, scales, words, word_scales, name):
+            acc = ps.tile([P, I], F32, name=name)
+            nc.tensor.matmul_mx(
+                out=acc[:],
+                lhsT=codes[:].bitcast(FP8X4),
+                lhsT_scale=scales[:],
+                rhs=words[:].bitcast(FP4X4),
+                rhs_scale=word_scales[:],
+                start=True,
+                stop=True,
+            )
+            return acc
+
+        g_grouped = interleave(g_raw, "g_grouped")
+        q_grouped = interleave(q_raw, "q_grouped")
+
+        g_scale = sb.tile([P, 1], F32, name="g_scale")
+        nc.scalar.activation(g_scale[:], w_col[:], ACT.Copy, scale=-512.0)
+        w512 = sb.tile([P, 1], F32, name="w512")
+        nc.scalar.activation(w512[:], w_col[:], ACT.Copy, scale=512.0)
+        g_bias = sb.tile([P, 1], F32, name="g_bias")
+        nc.scalar.activation(g_bias[:], delta_col[:], ACT.Copy, scale=w512[:])
+        neg_lse = sb.tile([P, 1], F32, name="neg_lse")
+        nc.scalar.activation(neg_lse[:], lse_col[:], ACT.Copy, scale=-1.0)
+
+        vs = gather(vs_pool, U8, "vs")
+        vw = gather(vw_pool, U16, "vw")
+        ks = gather(ks_pool, U8, "ks")
+        g_codes, g_scales = quantize(g_grouped, "g")
+        kw = gather(kw_pool, U16, "kw")
+        q_codes, q_scales = quantize(q_grouped, "q")
+        dp = product(g_codes, g_scales, vw, vs, "dp")
+        a = product(q_codes, q_scales, kw, ks, "a")
+
+        grad = sb.tile([P, I], F32, name="grad")
+        nc.scalar.activation(grad[:], dp[:], ACT.Identity, bias=g_bias[:], scale=g_scale[:])
+
+        halves = [slice(h * HALF, (h + 1) * HALF) for h in range(2)]
+        lists = [offsets[:, h * HALF // 16 : (h + 1) * HALF // 16] for h in range(2)]
+        picked_counts = [sb.tile([P, HALF], F32, name="picked_counts%d" % h) for h in range(2)]
+        neg_logit = [sb.tile([P, HALF], F32, name="neg_logit%d" % h) for h in range(2)]
+        weight = [sb.tile([P, HALF], F32, name="weight%d" % h) for h in range(2)]
+        grads = [grad[:, halves[h]] for h in range(2)]
+        for h in range(2):
+            nc.vector.tensor_copy(picked_counts[h][:], counts_pool[:].indirect(lists[h]))
+        for h in range(2):
+            nc.vector.scalar_tensor_tensor(
+                neg_logit[h][:], picked_counts[h][:], w_col[:], a[:, halves[h]], ALU.mult, ALU.subtract
+            )
+            nc.scalar.activation(weight[h][:], neg_logit[h][:], ACT.Exp, bias=neg_lse[:], scale=-1.0)
+        for h in range(2):
+            nc.vector.tensor_tensor(df[:].indirect(lists[h]), weight[h][:], grads[h], ALU.mult)
+
+        start = 0
+        for c, width in enumerate(OUT_WIDTHS):
+            cols = slice(start, start + width)
+            total = sb.tile([P, width], F32, name="total%d" % c)
+            nc.vector.tensor_tensor(total[:], df[:, cols], later_sb[:, cols], ALU.add)
+            nc.sync.dma_start(out[:, cols], total[:])
+            start = start + width

@@ -19,7 +19,7 @@ ACT = mybir.ActivationFunctionType
 P = 128
 PACK = 4
 HALF = I // 2
-OUT_WIDTHS = (512, 512, 512, 512)
+OUT_WIDTHS = (256, 512, 512, 512, 256)
 
 
 def tile_attend_gweariness_kernel(
@@ -31,18 +31,17 @@ def tile_attend_gweariness_kernel(
         ps = ctx.enter_context(tc.psum_pool(name="ps", bufs=1))
 
         offsets = sb.tile([P, I // 16], U16, name="offsets")
-        nc.sync.dma_start(offsets[:], offs)
 
-        def load_scales(src, name):
-            pool_scales = sb.tile([P, T], U8, name=name)
+        def load_scales(queue, src, name):
+            pool_scales = sb.tile([P, T], U8, name=name, align_bytes=64)
             nc.vector.memset(pool_scales[:].bitcast(I32), 0)
             rows = src[0].bitcast(I32)
             for r in range(4):
-                nc.sync.dma_start(pool_scales[:].bitcast(I32)[r:P:32, :], rows[r:16:4, :])
+                queue.dma_start(pool_scales[:].bitcast(I32)[r:P:32, :], rows[r:16:4, :])
             return pool_scales
 
         def load_words(src, name):
-            pool_words = sb.tile([P, T], U16, name=name)
+            pool_words = sb.tile([P, T], U16, name=name, align_bytes=64)
             nc.sync.dma_start(pool_words[:].bitcast(I32), src[0].bitcast(I32))
             return pool_words
 
@@ -56,61 +55,45 @@ def tile_attend_gweariness_kernel(
             nc.sync.dma_start(col[:], src)
             return col
 
-        warm = sb.tile([P, 1], F32, name="warm")
-        nc.gpsimd.memset(warm[:], 0.0)
-        warm_out = sb.tile([P, 1], F32, name="warm_out")
-        nc.scalar.activation(warm_out[:], warm[:], ACT.Exp)
-
-        vs_pool = load_scales(vals_scales, "vs_pool")
+        nc.sync.dma_start(offsets[:], offs)
+        vs_pool = load_scales(nc.sync, vals_scales, "vs_pool")
         vw_pool = load_words(vals_words, "vw_pool")
-        ks_pool = load_scales(keys_scales, "ks_pool")
+        w_col = load_column(weary, "w_col")
         g_raw = load_rows(gout, "g_raw")
         kw_pool = load_words(keys_words, "kw_pool")
         q_raw = load_rows(query, "q_raw")
-        w_col = load_column(weary, "w_col")
-        delta_col = load_column(delta, "delta_col")
-        lse_col = load_column(lse, "lse_col")
+        ks_pool = load_scales(nc.sync, keys_scales, "ks_pool")
         counts_pool = sb.tile([P, T], F32, name="counts_pool")
         nc.sync.dma_start(counts_pool[:], counts)
-        later_sb = sb.tile([P, T], F32, name="later_sb")
+        delta_col = load_column(delta, "delta_col")
+        lse_col = load_column(lse, "lse_col")
+        later_sb = sb.tile([P, T], F32, name="later_sb", tag="vw_pool", align_bytes=64)
         nc.sync.dma_start(later_sb[:], later)
 
         df = sb.tile([P, T], F32, name="df")
-        nc.vector.memset(df[:], 0.0)
+        nc.vector.memset(df[:].bitcast(I32), 0)
 
         def gather(pool_tile, dtype, name):
             picked = sb.tile([P, I], dtype, name=name, align_bytes=64)
             nc.vector.tensor_copy(picked[:], pool_tile[:].indirect(offsets[:]))
             return picked
 
-        def interleave(raw, name):
-            grouped = sb.tile([P, Q, PACK], BF16, name=name, align_bytes=64)
-            nc.scalar.copy(grouped[:], raw[:].rearrange("p j q -> p q j"))
-            return grouped
-
-        def quantize(grouped, name):
-            codes = sb.tile([P, Q], U32, name=name + "_codes", align_bytes=64)
-            scales = sb.tile([P, Q], U8, name=name + "_scales", align_bytes=64)
-            nc.vector.quantize_mx(
-                out=codes[:].bitcast(FP8X4), scales=scales[:], in_=grouped[:].rearrange("p q j -> p (q j)")
-            )
-            return codes, scales
-
         def product(codes, scales, words, word_scales, name):
-            acc = ps.tile([P, I], F32, name=name)
+            acc = ps.tile([P, words.shape[1]], F32, name=name)
             nc.tensor.matmul_mx(
                 out=acc[:],
-                lhsT=codes[:].bitcast(FP8X4),
-                lhsT_scale=scales[:],
-                rhs=words[:].bitcast(FP4X4),
-                rhs_scale=word_scales[:],
+                lhsT=codes.bitcast(FP8X4),
+                lhsT_scale=scales,
+                rhs=words.bitcast(FP4X4),
+                rhs_scale=word_scales,
                 start=True,
                 stop=True,
             )
             return acc
 
-        g_grouped = interleave(g_raw, "g_grouped")
-        q_grouped = interleave(q_raw, "q_grouped")
+        grouped = sb.tile([P, 2, Q, PACK], BF16, name="grouped", align_bytes=64)
+        nc.scalar.copy(grouped[:, 0], g_raw[:].rearrange("p j q -> p q j"))
+        nc.scalar.copy(grouped[:, 1], q_raw[:].rearrange("p j q -> p q j"))
 
         g_scale = sb.tile([P, 1], F32, name="g_scale")
         nc.scalar.activation(g_scale[:], w_col[:], ACT.Copy, scale=-512.0)
@@ -121,24 +104,34 @@ def tile_attend_gweariness_kernel(
         neg_lse = sb.tile([P, 1], F32, name="neg_lse")
         nc.scalar.activation(neg_lse[:], lse_col[:], ACT.Copy, scale=-1.0)
 
-        vs = gather(vs_pool, U8, "vs")
-        vw = gather(vw_pool, U16, "vw")
-        ks = gather(ks_pool, U8, "ks")
-        g_codes, g_scales = quantize(g_grouped, "g")
-        kw = gather(kw_pool, U16, "kw")
-        q_codes, q_scales = quantize(q_grouped, "q")
-        dp = product(g_codes, g_scales, vw, vs, "dp")
-        a = product(q_codes, q_scales, kw, ks, "a")
-
-        grad = sb.tile([P, I], F32, name="grad")
-        nc.scalar.activation(grad[:], dp[:], ACT.Identity, bias=g_bias[:], scale=g_scale[:])
-
         halves = [slice(h * HALF, (h + 1) * HALF) for h in range(2)]
         lists = [offsets[:, h * HALF // 16 : (h + 1) * HALF // 16] for h in range(2)]
-        picked_counts = [sb.tile([P, HALF], F32, name="picked_counts%d" % h) for h in range(2)]
+
+        def value_factor(h, vs_half):
+            nc.vector.tensor_copy(vs_half[:], vs_pool[:].indirect(lists[h]))
+            dp = product(codes[:, 0:Q], scales[:, 0:Q], vw[:, halves[h]], vs_half[:], "dp%d" % h)
+            grad = sb.tile([P, HALF], F32, name="grad%d" % h)
+            nc.scalar.activation(grad[:], dp[:], ACT.Identity, bias=g_bias[:], scale=g_scale[:])
+            return grad
+
+        vw = gather(vw_pool, U16, "vw")
+        kw = gather(kw_pool, U16, "kw")
+        codes = sb.tile([P, 2 * Q], U32, name="codes", align_bytes=64)
+        scales = sb.tile([P, 2 * Q], U8, name="scales", align_bytes=64)
+        nc.vector.quantize_mx(
+            out=codes[:].bitcast(FP8X4), scales=scales[:], in_=grouped[:].rearrange("p s q j -> p (s q j)")
+        )
+        vs_first = sb.tile([P, HALF], U8, name="vs_first", align_bytes=64)
+        grads = [value_factor(0, vs_first)]
+        ks = gather(ks_pool, U8, "ks")
+        a = product(codes[:, Q : 2 * Q], scales[:, Q : 2 * Q], kw[:], ks[:], "a")
+
+        picked_counts = [
+            sb.tile([P, HALF], F32, name="picked_counts%d" % h, tag=("kw_pool", "ks_pool")[h], align_bytes=64)
+            for h in range(2)
+        ]
         neg_logit = [sb.tile([P, HALF], F32, name="neg_logit%d" % h) for h in range(2)]
         weight = [sb.tile([P, HALF], F32, name="weight%d" % h) for h in range(2)]
-        grads = [grad[:, halves[h]] for h in range(2)]
         for h in range(2):
             nc.vector.tensor_copy(picked_counts[h][:], counts_pool[:].indirect(lists[h]))
         for h in range(2):
@@ -146,8 +139,10 @@ def tile_attend_gweariness_kernel(
                 neg_logit[h][:], picked_counts[h][:], w_col[:], a[:, halves[h]], ALU.mult, ALU.subtract
             )
             nc.scalar.activation(weight[h][:], neg_logit[h][:], ACT.Exp, bias=neg_lse[:], scale=-1.0)
+        vs_second = sb.tile([P, HALF], U8, name="vs_second", tag="kw_pool", align_bytes=64)
+        grads.append(value_factor(1, vs_second))
         for h in range(2):
-            nc.vector.tensor_tensor(df[:].indirect(lists[h]), weight[h][:], grads[h], ALU.mult)
+            nc.vector.tensor_tensor(df[:].indirect(lists[h]), weight[h][:], grads[h][:], ALU.mult)
 
         start = 0
         for c, width in enumerate(OUT_WIDTHS):

from contextlib import ExitStack

import concourse.mybir as mybir

D, E, T, I, Q = 512, 512, 2048, 512, 128
FLOPS = 2 * Q * I * (D + E)

F32 = mybir.dt.float32
BF16 = mybir.dt.bfloat16
I32 = mybir.dt.int32
U32 = mybir.dt.uint32
U16 = mybir.dt.uint16
U8 = mybir.dt.uint8
FP8X4 = mybir.dt.float8_e4m3fn_x4
FP4X4 = mybir.dt.float4_e2m1fn_x4
ALU = mybir.AluOpType
ACT = mybir.ActivationFunctionType

P = 128
PACK = 4
HALF = I // 2
OUT_WIDTHS = (256, 512, 512, 512, 256)


def tile_attend_gweariness_kernel(
    tc, query, keys_words, keys_scales, counts, weary, gout, vals_words, vals_scales, lse, delta, later, offs, out
):
    nc = tc.nc
    with ExitStack() as ctx:
        sb = ctx.enter_context(tc.tile_pool(name="sb", bufs=1))
        ps = ctx.enter_context(tc.psum_pool(name="ps", bufs=1))

        offsets = sb.tile([P, I // 16], U16, name="offsets")

        def load_scales(queue, src, name):
            pool_scales = sb.tile([P, T], U8, name=name, align_bytes=64)
            nc.vector.memset(pool_scales[:].bitcast(I32), 0)
            rows = src[0].bitcast(I32)
            for r in range(4):
                queue.dma_start(pool_scales[:].bitcast(I32)[r:P:32, :], rows[r:16:4, :])
            return pool_scales

        def load_words(src, name):
            pool_words = sb.tile([P, T], U16, name=name, align_bytes=64)
            nc.sync.dma_start(pool_words[:].bitcast(I32), src[0].bitcast(I32))
            return pool_words

        def load_rows(src, name):
            raw = sb.tile([P, PACK, Q], F32, name=name)
            nc.sync.dma_start(raw[:], src.rearrange("(p j) q -> p j q", j=PACK))
            return raw

        def load_column(src, name):
            col = sb.tile([P, 1], F32, name=name)
            nc.sync.dma_start(col[:], src)
            return col

        nc.sync.dma_start(offsets[:], offs)
        vs_pool = load_scales(nc.sync, vals_scales, "vs_pool")
        vw_pool = load_words(vals_words, "vw_pool")
        w_col = load_column(weary, "w_col")
        g_raw = load_rows(gout, "g_raw")
        kw_pool = load_words(keys_words, "kw_pool")
        q_raw = load_rows(query, "q_raw")
        ks_pool = load_scales(nc.sync, keys_scales, "ks_pool")
        counts_pool = sb.tile([P, T], F32, name="counts_pool")
        nc.sync.dma_start(counts_pool[:], counts)
        delta_col = load_column(delta, "delta_col")
        lse_col = load_column(lse, "lse_col")
        later_sb = sb.tile([P, T], F32, name="later_sb", tag="vw_pool", align_bytes=64)
        nc.sync.dma_start(later_sb[:], later)

        df = sb.tile([P, T], F32, name="df")
        nc.vector.memset(df[:].bitcast(I32), 0)

        def gather(pool_tile, dtype, name):
            picked = sb.tile([P, I], dtype, name=name, align_bytes=64)
            nc.vector.tensor_copy(picked[:], pool_tile[:].indirect(offsets[:]))
            return picked

        def product(codes, scales, words, word_scales, name):
            acc = ps.tile([P, words.shape[1]], F32, name=name)
            nc.tensor.matmul_mx(
                out=acc[:],
                lhsT=codes.bitcast(FP8X4),
                lhsT_scale=scales,
                rhs=words.bitcast(FP4X4),
                rhs_scale=word_scales,
                start=True,
                stop=True,
            )
            return acc

        grouped = sb.tile([P, 2, Q, PACK], BF16, name="grouped", align_bytes=64)
        nc.scalar.copy(grouped[:, 0], g_raw[:].rearrange("p j q -> p q j"))
        nc.scalar.copy(grouped[:, 1], q_raw[:].rearrange("p j q -> p q j"))

        g_scale = sb.tile([P, 1], F32, name="g_scale")
        nc.scalar.activation(g_scale[:], w_col[:], ACT.Copy, scale=-512.0)
        w512 = sb.tile([P, 1], F32, name="w512")
        nc.scalar.activation(w512[:], w_col[:], ACT.Copy, scale=512.0)
        g_bias = sb.tile([P, 1], F32, name="g_bias")
        nc.scalar.activation(g_bias[:], delta_col[:], ACT.Copy, scale=w512[:])
        neg_lse = sb.tile([P, 1], F32, name="neg_lse")
        nc.scalar.activation(neg_lse[:], lse_col[:], ACT.Copy, scale=-1.0)

        halves = [slice(h * HALF, (h + 1) * HALF) for h in range(2)]
        lists = [offsets[:, h * HALF // 16 : (h + 1) * HALF // 16] for h in range(2)]

        def value_factor(h, vs_half):
            nc.vector.tensor_copy(vs_half[:], vs_pool[:].indirect(lists[h]))
            dp = product(codes[:, 0:Q], scales[:, 0:Q], vw[:, halves[h]], vs_half[:], "dp%d" % h)
            grad = sb.tile([P, HALF], F32, name="grad%d" % h)
            nc.scalar.activation(grad[:], dp[:], ACT.Identity, bias=g_bias[:], scale=g_scale[:])
            return grad

        vw = gather(vw_pool, U16, "vw")
        kw = gather(kw_pool, U16, "kw")
        codes = sb.tile([P, 2 * Q], U32, name="codes", align_bytes=64)
        scales = sb.tile([P, 2 * Q], U8, name="scales", align_bytes=64)
        nc.vector.quantize_mx(
            out=codes[:].bitcast(FP8X4), scales=scales[:], in_=grouped[:].rearrange("p s q j -> p (s q j)")
        )
        vs_first = sb.tile([P, HALF], U8, name="vs_first", align_bytes=64)
        grads = [value_factor(0, vs_first)]
        ks = gather(ks_pool, U8, "ks")
        a = product(codes[:, Q : 2 * Q], scales[:, Q : 2 * Q], kw[:], ks[:], "a")

        picked_counts = [
            sb.tile([P, HALF], F32, name="picked_counts%d" % h, tag=("kw_pool", "ks_pool")[h], align_bytes=64)
            for h in range(2)
        ]
        neg_logit = [sb.tile([P, HALF], F32, name="neg_logit%d" % h) for h in range(2)]
        weight = [sb.tile([P, HALF], F32, name="weight%d" % h) for h in range(2)]
        for h in range(2):
            nc.vector.tensor_copy(picked_counts[h][:], counts_pool[:].indirect(lists[h]))
        for h in range(2):
            nc.vector.scalar_tensor_tensor(
                neg_logit[h][:], picked_counts[h][:], w_col[:], a[:, halves[h]], ALU.mult, ALU.subtract
            )
            nc.scalar.activation(weight[h][:], neg_logit[h][:], ACT.Exp, bias=neg_lse[:], scale=-1.0)
        vs_second = sb.tile([P, HALF], U8, name="vs_second", tag="kw_pool", align_bytes=64)
        grads.append(value_factor(1, vs_second))
        for h in range(2):
            nc.vector.tensor_tensor(df[:].indirect(lists[h]), weight[h][:], grads[h][:], ALU.mult)

        start = 0
        for c, width in enumerate(OUT_WIDTHS):
            cols = slice(start, start + width)
            total = sb.tile([P, width], F32, name="total%d" % c)
            nc.vector.tensor_tensor(total[:], df[:, cols], later_sb[:, cols], ALU.add)
            nc.sync.dma_start(out[:, cols], total[:])
            start = start + width
